import numpy as np, ml_dtypes
CORES = [2,3,42,43,82,83,122,123]
N = 8
import mx_ref
BF = ml_dtypes.bfloat16
def entries(a):
    return np.ascontiguousarray(a.T).reshape(-1)
def table(e):
    return np.ascontiguousarray(np.reshape(e, (-1, 16)).T).astype(np.int32)
def cols(t, e):
    v = np.concatenate([t.reshape(128, -1, 4), np.zeros((128, 1, 4), BF)], axis=1)
    return np.ascontiguousarray(v[:, e]).reshape(128, -1)
def f(rng, *shape):
    return mx_ref.flush((rng.standard_normal(shape, dtype=np.float32) * np.exp2(rng.integers(-2, 3, shape[:-1] + (1,)))).astype(BF))
def wide(rng, *shape, cols=0):
    v = rng.standard_normal(shape, dtype=np.float32) * np.exp2(rng.integers(-12, 13, shape)).astype(np.float32)
    if cols: v *= np.repeat(np.exp2(rng.integers(-cols, cols + 1, shape[:-2] + (1, shape[-1] // 4))) * (rng.random(shape[:-2] + (1, shape[-1] // 4)) > 0.0625), 4, axis=-1).astype(np.float32)
    return mx_ref.flush(v.astype(BF))
T, CAPP = 512, 96
def lists(rng, full=False, skew=False, single=False, back=False):
    if full:
        v = rng.permutation(([CAPP] * (T // CAPP) + [T % CAPP] + [0] * N)[:N])
        n = v[(np.arange(N)[None, :] - np.arange(N)[:, None]) % N][rng.permutation(N)][:, rng.permutation(N)]
    else:
        n = np.full((N, N), T // N)
        for _ in range(20 * N):
            (s, t), (d, e) = rng.permutation(N)[:2], rng.permutation(N)[:2]
            k = rng.integers(0, min(n[s, d], n[t, e], CAPP - n[s, e], CAPP - n[t, d]) + 1)
            n[s, d] -= k; n[t, e] -= k; n[s, e] += k; n[t, d] += k
    a = np.full((N, N * CAPP), -1)
    for s in range(N):
        parts = np.split(rng.permutation(T), np.cumsum(n[s])[:-1])
        for d in range(N): a[s, d * CAPP + rng.permutation(CAPP)[:n[s, d]]] = parts[d]
    p, u, o = [], [], []
    for r in range(N):
        used = np.flatnonzero(a[:, r * CAPP:(r + 1) * CAPP].reshape(-1) >= 0)
        p.append(table(used[::-1] if back else rng.permutation(used)))
        h = rng.integers(0, N)
        c = rng.integers(0, 2, N) if full else (np.full(N, -1) if rng.random() < 0.5 else rng.integers(0, 2, N)) if single else rng.integers(-1, 2, N)
        if c[h] < 0: c[h] = rng.integers(0, 2)
        named = np.flatnonzero(c >= 0)
        if single: named = np.array([h])
        if skew:
            m = rng.integers(T // 2 + 1, T + 1)
            e = np.sort(np.concatenate([np.full(m, h), rng.choice(named, T - m)]))
        elif full: e = np.sort(np.concatenate([named, rng.choice(named, T - N)]))
        else: e = np.repeat(named, np.diff(np.concatenate([[0], np.sort(rng.integers(0, T + 1, len(named) - 1)), [T]])))
        u.append(table(np.concatenate([c, np.full(16 - N, -1)]))); o.append(table(e))
    return {"send": np.stack([table(k) for k in a]), "place": np.stack(p), "sel": np.stack(u), "of": np.stack(o)}
def setup_inputs(rng):
    return {"x": f(rng, N, 128, 4 * T), "w": f(rng, N, 256, 512), **lists(rng)}
def setup_inputs_full(rng):
    return {**setup_inputs(rng), **lists(rng, full=True)}
def setup_inputs_reversed(rng):
    return {**setup_inputs(rng), **lists(rng, back=True)}
def setup_inputs_single(rng):
    return {**setup_inputs(rng), **lists(rng, single=True)}
def setup_inputs_skew(rng):
    return {**setup_inputs(rng), **lists(rng, skew=True)}
def setup_inputs_spread(rng):
    d = setup_inputs(rng); d["x"] = wide(rng, N, 128, 4 * T, cols=8); return d
def check_inputs(d):
    b = []
    for k in ("x", "w"):
        a = np.abs(d[k].astype(np.float32))
        if not ((a == 0) | ((a >= 2.0 ** -30) & (a <= 2.0 ** 30))).all(): b.append(k)
    sends = np.stack([entries(d["send"][r]) for r in range(N)])
    for r in range(N):
        c, p, u, e = sends[r], entries(d["place"][r]), entries(d["sel"][r]), entries(d["of"][r])
        if c.min() < -1 or not np.array_equal(np.sort(c[c >= 0]), np.arange(T)): b.append("send")
        if not np.array_equal(np.sort(p), np.flatnonzero(sends[:, r * CAPP:(r + 1) * CAPP].reshape(-1) >= 0)): b.append("place")
        if u.min() < -1 or u.max() > 1 or (u[N:] != -1).any(): b.append("sel")
        if e.min() < 0 or e.max() >= N or (np.diff(e) < 0).any() or (u[e] < 0).any(): b.append("of")
    return b
def reference(x, w, send, place, sel, of):
    W = [[mx_ref.quantize(w[h][128 * m:128 * m + 128]) for m in range(2)] for h in range(N)]
    y = np.zeros((N, 128, T), np.float32)
    for r in range(N):
        slots = np.concatenate([cols(x[s], entries(send[s])[r * CAPP:(r + 1) * CAPP]) for s in range(N)], axis=1)
        X = mx_ref.quantize(cols(slots, entries(place[r])))
        u, e = entries(sel[r]), entries(of[r])
        for h in range(N):
            i = e == h
            if i.any(): y[r][:, i] = mx_ref.matmul(W[h][u[h]], X)[:, i]
    return {"y": y}

@@ -1,0 +1,305 @@
+from concourse.bass import DstId, RemoteDMATransfer
+from concourse.mybir import dt, AluOpType, ActivationFunctionType
+
+N, TC, CAPP, NE = 8, 512, 96, 128
+SLOTS = N * CAPP
+HALF = SLOTS // 2
+CODE = "float8_e4m3fn_x4"
+
+SCRATCH = {
+    "srow": ("sbuf", [1, 16], "int32"), "sbc": ("sbuf", [128, 16], "int32"), "sf": ("sbuf", [128, 16], "float32"),
+    "selv": ("sbuf", [128, N], "float32"),
+    "snd": ("sbuf", [128, SLOTS // 16], "int32"), "xo": ("sbuf", [128, SLOTS // 16], "uint16"),
+    "ip": ("sbuf", [128, 32], "int32"), "ia": ("sbuf", [128, 32], "int32"), "ic": ("sbuf", [128, 32], "int32"),
+    "base": ("sbuf", [128, 32], "float32"), "wo": ("sbuf", [128, 32 * N], "uint16"),
+    "pl": ("sbuf", [128, 32], "int32"), "ofl": ("sbuf", [128, 32], "int32"),
+    "i1": ("sbuf", [128, 32], "float32"), "i2": ("sbuf", [128, 32], "float32"), "idx": ("sbuf", [128, 32], "uint16"),
+    "xt": ("sbuf", [128, 4 * TC], "bfloat16"), "xg": ("sbuf", [128, 4 * SLOTS], "bfloat16"),
+    "xq": ("sbuf", [128, SLOTS], CODE), "xs": ("sbuf", [128, SLOTS], "uint8"),
+    "wt": ("sbuf", [128, 8 * NE], "bfloat16"), "wg": ("sbuf", [128, 4 * NE * N], "bfloat16"),
+    "wq": ("sbuf", [128, NE * N], CODE), "ws": ("sbuf", [128, NE * N], "uint8"),
+    "xr": ("sbuf", [128, SLOTS], CODE), "xrs": ("sbuf", [128, SLOTS], "uint8"),
+    "ew": ("sbuf", [128, NE * N], CODE), "es": ("sbuf", [128, NE * N], "uint8"),
+    "hx": ("sbuf", [128, 2 * CAPP], CODE), "hxs": ("sbuf", [128, 2 * CAPP], "uint8"),
+    "hw": ("sbuf", [128, 2 * NE], CODE), "hws": ("sbuf", [128, 2 * NE], "uint8"),
+    "ps": ("psum", [128, 4096], "float32"), "res": ("sbuf", [128, N * SLOTS], "float32"),
+    "yt": ("sbuf", [128, TC], "float32"),
+}
+SEMAPHORES = (["ldsel", "ldsnd", "ldx", "ldw", "ldi", "rep", "own", "yd",
+               "iot", "ian", "bas", "selb", "sfd", "selq", "seli", "xoa", "xob", "xga", "xgb", "xqa", "xqb",
+               "ix1", "ix2", "ix3", "woa", "wob", "woc", "wga", "wgb", "wgc", "wqa", "wqb", "wqc",
+               "xin", "cpl", "gv", "gs", "sent", "hxc", "hxp", "hwc", "hwp"]
+              + ["we%d" % k for k in range(N)] + ["ma%d" % k for k in range(N)] + ["mb%d" % k for k in range(N)]
+              + ["cp%d" % k for k in range(4)])
+
+
+def bits(es):
+    m = 0
+    for e in es:
+        m |= 1 << e
+    return m
+
+
+def plan(core, T, topo):
+    cores = list(T.cores)
+    chips = []
+    for c in cores:
+        if topo.chip(c) not in chips:
+            chips.append(topo.chip(c))
+    pair = [[r for r in range(N) if topo.chip(cores[r]) == h] for h in chips]
+    k = chips.index(topo.chip(core))
+    rest = [(k + i) % len(chips) for i in range(1, len(chips))]
+    same = [i for i in rest if topo.same_plane(chips[i], chips[k])]
+    cross = [i for i in rest if i not in same]
+    p = {"O": pair[k], "S": pair[same[0]], "P": pair[cross[0]], "Q": pair[cross[1]]}
+    mine = pair[k].index(T.rank_of(core))
+    away = [c for c in topo.cores_of(core) if c not in cores and topo.die(c) != topo.die(core)]
+    owners = [c for c in away if all(topo.may_write(c, cores[d]) for d in p["Q"])]
+    p["A"] = owners[mine]
+    p["B"] = [c for c in away if c not in owners][mine]
+    return p
+
+
+def dst_of(topo, c):
+    rid, pid, _ = topo.addr(c)
+    return DstId(rid=rid, pnc=pid)
+
+
+def u8(ap):
+    return ap.bitcast(dt.uint8)
+
+
+def helper_program(g, core, T, topo):
+    for r in range(N):
+        p = plan(T.cores[r], T, topo)
+        if core == p["A"]:
+            pair, both = p["Q"], True
+        elif core == p["B"]:
+            pair, both = p["S"], False
+        else:
+            continue
+        off = topo.engines(core, T.cores[pair[0]])
+        h = len(off) // 2
+        masks = [bits(off[:h]), bits(off[h:])]
+        count = [0]
+
+        def hand(sem, n, src, w, dst, at, rsem, code):
+            g.wait_ge(sem, n)
+            view = u8 if code else (lambda v: v)
+            g.remote_dma_fused([RemoteDMATransfer(
+                dst_ids=[dst_of(topo, T.cores[d])], dma_engine_mask=masks[i], remote_sem=rsem,
+                src=view(src[:, i * w:(i + 1) * w]), dst=view(dst[:, at * w:(at + 1) * w])) for i, d in enumerate(pair)],
+                local_sem=T.sem.sent)
+            count[0] += 2 * h
+
+        on = len(topo.engines(core, T.cores[r])) - len(off)
+        hand(T.sem.hxc, on // 2, T.hx, CAPP, T.xr, r, T.sem.xin, True)
+        hand(T.sem.hxp, on // 2, T.hxs, CAPP, T.xrs, r, T.sem.xin, False)
+        if both:
+            hand(T.sem.hwc, on, T.hw, NE, T.ew, r, T.sem["we%d" % r], True)
+            hand(T.sem.hwp, on, T.hws, NE, T.es, r, T.sem["we%d" % r], False)
+        g.wait_ge(T.sem.sent, count[0])
+
+
+def rank_program(g, core, T, topo):
+    r = T.rank_of(core)
+    if r is None:
+        return helper_program(g, core, T, topo)
+    V, S, PE, Y = g.vector, g.scalar, g.tensor, g.sync
+    sem, A = T.sem, AluOpType
+    COPY = ActivationFunctionType.Copy
+    cores = T.cores
+    p = plan(core, T, topo)
+    partner = [d for d in p["O"] if d != r][0]
+    order = p["Q"] + p["S"] + p["O"] + p["P"]
+    pos = {d: k for k, d in enumerate(order)}
+    off = topo.engines(core, cores[p["P"][0]])
+    on = [e for e in topo.engines(core, cores[partner]) if e not in off]
+    o4, n4 = len(off) // 2, len(on) // 2
+    offm, onm = [bits(off[:o4]), bits(off[o4:])], [bits(on[:n4]), bits(on[n4:])]
+
+    Y.dma_start(T.srow[0:1, :], T.sel[:]).then_inc(sem.ldsel, 16)
+    for k in range(8):
+        q = Y if k % 2 else S
+        q.dma_start(T.snd[16 * k:16 * k + 16, :], T.send[:]).then_inc(sem.ldsnd, 16)
+    Y.dma_start(T.xt[0:64, :], T.x[0:64, :]).then_inc(sem.ldx, 16)
+    S.dma_start(T.xt[64:128, :], T.x[64:128, :]).then_inc(sem.ldx, 16)
+    Y.dma_start(T.wt[:, 0:4 * NE], T.w[0:128, :]).then_inc(sem.ldw, 16)
+    S.dma_start(T.wt[:, 4 * NE:8 * NE], T.w[128:256, :]).then_inc(sem.ldw, 16)
+    Y.dma_start(T.pl[0:16, :], T.place[:]).then_inc(sem.ldi, 16)
+    Y.dma_start(T.ofl[0:16, :], T.of[:]).then_inc(sem.ldi, 16)
+
+    g.iota(T.ip[:], [[0, 32]], 0, 1).then_inc(sem.iot, 1)
+    g.iota(T.ic[:], [[16, 32]], 0, 0).then_inc(sem.iot, 1)
+    g.wait_ge(sem.ldsel, 16)
+    g.partition_broadcast(T.sbc[:], T.srow[0:1, :], 128).then_inc(sem.selb, 1)
+
+    V.wait_ge(sem.iot, 2)
+    V.tensor_scalar(T.ia[:], T.ip[:], 15, None, A.bitwise_and).then_inc(sem.ian, 1)
+    V.wait_ge(sem.ian, 1)
+    V.tensor_tensor(T.base[:], T.ia[:], T.ic[:], A.add).then_inc(sem.bas, 1)
+    V.wait_ge(sem.selb, 1)
+    V.tensor_scalar(T.sf[:], T.sbc[:], float(4 * NE), 0.0, A.mult, A.max).then_inc(sem.sfd, 1)
+
+    sent = 0
+    tr = []
+    share = {d: [e] for d, e in zip(p["S"] + p["Q"], off[0:4])}
+    share.update({d: off[4 + 2 * i:6 + 2 * i] for i, d in enumerate(p["P"])})
+    share[partner] = on
+    for d in p["P"] + p["S"] + p["Q"] + [partner]:
+        first = r in plan(cores[d], T, topo)["Q"]
+        tr.append(RemoteDMATransfer(dst_ids=[dst_of(topo, cores[d])], dma_engine_mask=bits(share[d]),
+                                    remote_sem=sem.selq if first else sem.seli,
+                                    src=T.sf[:, d:d + 1], dst=T.selv[:, r:r + 1]))
+        sent += len(share[d])
+    g.wait_ge(sem.sfd, 1)
+    g.remote_dma_fused(tr, local_sem=sem.sent)
+    nq, ni = 2 * 2, 4 * 1 + len(on)
+
+    V.wait_ge(sem.ldsnd, 128)
+    for k in range(4):
+        d = order[2 * k]
+        V.tensor_scalar(T.xo[:, 12 * k:12 * k + 12], T.snd[:, 6 * d:6 * d + 12], 4.0, 0.0, A.mult, A.max
+                        ).then_inc(sem.xoa if k < 2 else sem.xob, 1)
+    for q, ts in ((V, (0, 1)), (S, (2, 3))):
+        q.wait_ge(sem.ldx, 32)
+        for b, (so, sg, sq) in enumerate(((sem.xoa, sem.xga, sem.xqa), (sem.xob, sem.xgb, sem.xqb))):
+            a = HALF * b
+            q.wait_ge(so, 2)
+            for t in ts:
+                out = T.xg[:, 4 * a + t:4 * (a + HALF):4]
+                win = T.xt[:, t:4 * TC].indirect(T.xo[:, a // 16:(a + HALF) // 16])
+                if q is V:
+                    V.tensor_copy(out, win).then_inc(sg, 1)
+                else:
+                    S.activation(out, win, COPY).then_inc(sg, 1)
+            if q is V:
+                V.wait_ge(sg, 4)
+                V.quantize_mx(T.xq[:, a:a + HALF], T.xs[:, a:a + HALF], T.xg[:, 4 * a:4 * (a + HALF)]).then_inc(sq, 1)
+
+    a = CAPP * pos[r]
+    Y.wait_ge(sem.xqb, 1)
+    Y.dma_start(u8(T.xr[:, CAPP * r:CAPP * (r + 1)]), u8(T.xq[:, a:a + CAPP])).then_inc(sem.own, 16)
+    Y.dma_start(T.xrs[:, CAPP * r:CAPP * (r + 1)], T.xs[:, a:a + CAPP]).then_inc(sem.own, 16)
+
+    V.wait_ge(sem.ldi, 32)
+    V.tensor_scalar(T.i1[0:16, :], T.ofl[0:16, :], float(SLOTS), None, A.mult).then_inc(sem.ix1, 1)
+    V.wait_ge(sem.ix1, 1)
+    V.tensor_tensor(T.i2[0:16, :], T.i1[0:16, :], T.pl[0:16, :], A.add).then_inc(sem.ix2, 1)
+    V.wait_ge(sem.ix2, 1)
+    V.tensor_copy(T.idx[0:16, :], T.i2[0:16, :]).then_inc(sem.ix3, 1)
+    Y.wait_ge(sem.ix3, 1)
+    for k in range(1, 8):
+        Y.dma_start(T.idx[16 * k:16 * k + 16, :], T.idx[0:16, :]).then_inc(sem.rep, 16)
+
+    def offs(d, s):
+        col = T.sf[:, r:r + 1] if d == r else T.selv[:, d:d + 1]
+        k = pos[d]
+        V.tensor_scalar(T.wo[:, 32 * k:32 * k + 32], T.base[:], col, None, A.add).then_inc(s, 1)
+
+    def pick(q, ks, s):
+        out = T.wg[:, 4 * NE * ks[0]:4 * NE * (ks[-1] + 1)]
+        win = T.wt[:].indirect(T.wo[:, 32 * ks[0]:32 * (ks[-1] + 1)])
+        if q is V:
+            V.tensor_copy(out, win).then_inc(s, 1)
+        else:
+            S.activation(out, win, COPY).then_inc(s, 1)
+
+    def pack(k, n, s):
+        V.quantize_mx(T.wq[:, NE * k:NE * (k + n)], T.ws[:, NE * k:NE * (k + n)],
+                      T.wg[:, 4 * NE * k:4 * NE * (k + n)]).then_inc(s, 1)
+
+    V.wait_ge(sem.bas, 1)
+    V.wait_ge(sem.ldw, 32)
+    S.wait_ge(sem.ldw, 32)
+    V.wait_ge(sem.selq, nq)
+    for (vk, sk, so, sg, sq) in (([0], [1], sem.woa, sem.wga, sem.wqa), ([2, 3], [4, 5], sem.wob, sem.wgb, sem.wqb),
+                                 ([6], [7], sem.woc, sem.wgc, sem.wqc)):
+        for k in sk + vk:
+            offs(order[k], so)
+        n = len(vk + sk)
+        S.wait_ge(so, n)
+        pick(S, sk, sg)
+        V.wait_ge(so, n)
+        pick(V, vk, sg)
+        V.wait_ge(sg, 2)
+        pack(vk[0], n, sq)
+        if n == 2 and vk[0] == 0:
+            V.wait_ge(sem.seli, ni)
+
+    def send(items, local):
+        g.remote_dma_fused(items, local_sem=local)
+
+    def tx(c, mask, rs, src, dst):
+        return RemoteDMATransfer(dst_ids=[dst_of(topo, c)], dma_engine_mask=mask, remote_sem=rs, src=src, dst=dst)
+
+    def xcol(d, n=1):
+        return CAPP * pos[d], CAPP * (pos[d] + n)
+
+    x0, x1 = xcol(p["Q"][0], 2)
+    z0, z1 = xcol(p["S"][0], 2)
+    g.wait_ge(sem.xqa, 1)
+    send([tx(p["A"], onm[0], sem.hxc, u8(T.xq[:, x0:x1]), u8(T.hx[:])),
+          tx(p["B"], onm[1], sem.hxc, u8(T.xq[:, z0:z1]), u8(T.hx[:]))], sem.sent)
+    send([tx(p["A"], onm[0], sem.hxp, T.xs[:, x0:x1], T.hxs[:]),
+          tx(p["B"], onm[1], sem.hxp, T.xs[:, z0:z1], T.hxs[:])], sem.sent)
+    sent += 2 * len(on)
+
+    def spread(pair, withp, src, ssrc, dst, sdst, w, rs):
+        tgt = [(d, offm[i]) for i, d in enumerate(pair)] + ([(partner, bits(on))] if withp else [])
+        for code in (True, False):
+            view = u8 if code else (lambda v: v)
+            s, t = (src, dst) if code else (ssrc, sdst)
+            send([tx(cores[d], m, rs, view(s[:, w * pos[d]:w * (pos[d] + 1)]), view(t[:, w * r:w * (r + 1)]))
+                  for d, m in tgt], sem.sent)
+        return 2 * (len(off) + (len(on) if withp else 0))
+
+    g.wait_ge(sem.xqb, 1)
+    sent += spread(p["P"], True, T.xq, T.xs, T.xr, T.xrs, CAPP, sem.xin)
+    we = sem["we%d" % r]
+    g.wait_ge(sem.wqa, 1)
+    k = NE * pos[p["Q"][0]]
+    send([tx(p["A"], bits(on), sem.hwc, u8(T.wq[:, k:k + 2 * NE]), u8(T.hw[:]))], sem.sent)
+    send([tx(p["A"], bits(on), sem.hwp, T.ws[:, k:k + 2 * NE], T.hws[:])], sem.sent)
+    sent += 2 * len(on)
+    g.wait_ge(sem.wqb, 1)
+    sent += spread(p["S"], True, T.wq, T.ws, T.ew, T.es, NE, we)
+    g.wait_ge(sem.wqc, 1)
+    sent += spread(p["P"], False, T.wq, T.ws, T.ew, T.es, NE, we)
+    g.wait_ge(sem.sent, sent)
+
+    todo = [r, partner] + p["S"] + p["Q"] + p["P"]
+    PE.wait_ge(sem.own, 32)
+    PE.wait_ge(sem.xin, 6 * 2 * o4 + 2 * len(on))
+    for k, h in enumerate(todo):
+        if h == r:
+            PE.wait_ge(sem.wqb, 1)
+            st, ss = T.wq[:, NE * pos[r]:NE * (pos[r] + 1)], T.ws[:, NE * pos[r]:NE * (pos[r] + 1)]
+        else:
+            PE.wait_ge(sem["we%d" % h], 2 * (len(on) if h == partner else o4))
+            st, ss = T.ew[:, NE * h:NE * (h + 1)], T.es[:, NE * h:NE * (h + 1)]
+        if k >= 4:
+            PE.wait_ge(sem["cp%d" % (k - 4)], 2)
+        b = 1024 * (k % 4)
+        PE.matmul_mx(T.ps[:, b:b + HALF], st, ss, T.xr[:, 0:HALF], T.xrs[:, 0:HALF], True, True
+                     ).then_inc(sem["ma%d" % k], 1)
+        PE.matmul_mx(T.ps[:, b + 512:b + 512 + HALF], st, ss, T.xr[:, HALF:SLOTS], T.xrs[:, HALF:SLOTS], True, True
+                     ).then_inc(sem["mb%d" % k], 1)
+        done = sem["cp%d" % k] if k < 4 else sem.cpl
+        V.wait_ge(sem["ma%d" % k], 1)
+        V.tensor_copy(T.res[:, SLOTS * h:SLOTS * h + HALF], T.ps[:, b:b + HALF]).then_inc(done, 1)
+        S.wait_ge(sem["mb%d" % k], 1)
+        S.activation(T.res[:, SLOTS * h + HALF:SLOTS * (h + 1)], T.ps[:, b + 512:b + 512 + HALF], COPY).then_inc(done, 1)
+
+    h = TC // 2
+    for q in (V, S):
+        q.wait_ge(sem.rep, 112)
+        q.wait_ge(sem.ix3, 1)
+        q.wait_ge(sem.cpl, 8)
+    V.tensor_copy(T.yt[:, 0:h], T.res[:].indirect(T.idx[:, 0:16])).then_inc(sem.gv, 1)
+    S.activation(T.yt[:, h:TC], T.res[:].indirect(T.idx[:, 16:32]), COPY).then_inc(sem.gs, 1)
+    Y.wait_ge(sem.gv, 1)
+    Y.dma_start(T.y[:, 0:h], T.yt[:, 0:h]).then_inc(sem.yd, 16)
+    S.wait_ge(sem.gs, 1)
+    S.dma_start(T.y[:, h:TC], T.yt[:, h:TC]).then_inc(sem.yd, 16)
+    Y.wait_ge(sem.yd, 32)

@@ -6,31 +6,26 @@ SLOTS = N * CAPP
 HALF = SLOTS // 2
 CODE = "float8_e4m3fn_x4"
 
+
+def sb(n, t, p=128):
+    return ("sbuf", [p, n], t)
+
+
 SCRATCH = {
-    "srow": ("sbuf", [1, 16], "int32"), "sbc": ("sbuf", [128, 16], "int32"), "sf": ("sbuf", [128, 16], "float32"),
-    "selv": ("sbuf", [128, N], "float32"),
-    "snd": ("sbuf", [128, SLOTS // 16], "int32"), "xo": ("sbuf", [128, SLOTS // 16], "uint16"),
-    "ip": ("sbuf", [128, 32], "int32"), "ia": ("sbuf", [128, 32], "int32"), "ic": ("sbuf", [128, 32], "int32"),
-    "base": ("sbuf", [128, 32], "float32"), "wo": ("sbuf", [128, 32 * N], "uint16"),
-    "pl": ("sbuf", [128, 32], "int32"), "ofl": ("sbuf", [128, 32], "int32"),
-    "i1": ("sbuf", [128, 32], "float32"), "i2": ("sbuf", [128, 32], "float32"), "idx": ("sbuf", [128, 32], "uint16"),
-    "xt": ("sbuf", [128, 4 * TC], "bfloat16"), "xg": ("sbuf", [128, 4 * SLOTS], "bfloat16"),
-    "xq": ("sbuf", [128, SLOTS], CODE), "xs": ("sbuf", [128, SLOTS], "uint8"),
-    "wt": ("sbuf", [128, 8 * NE], "bfloat16"), "wg": ("sbuf", [128, 4 * NE * N], "bfloat16"),
-    "wq": ("sbuf", [128, NE * N], CODE), "ws": ("sbuf", [128, NE * N], "uint8"),
-    "xr": ("sbuf", [128, SLOTS], CODE), "xrs": ("sbuf", [128, SLOTS], "uint8"),
-    "ew": ("sbuf", [128, NE * N], CODE), "es": ("sbuf", [128, NE * N], "uint8"),
-    "hx": ("sbuf", [128, 2 * CAPP], CODE), "hxs": ("sbuf", [128, 2 * CAPP], "uint8"),
-    "hw": ("sbuf", [128, 2 * NE], CODE), "hws": ("sbuf", [128, 2 * NE], "uint8"),
-    "ps": ("psum", [128, 4096], "float32"), "res": ("sbuf", [128, N * SLOTS], "float32"),
-    "yt": ("sbuf", [128, TC], "float32"),
+    "srow": sb(16, "int32", 1), "sbc": sb(16, "int32"), "sf": sb(16, "float32"), "selv": sb(N, "float32"),
+    "snd": sb(SLOTS // 16, "int32"), "xo": sb(SLOTS // 16, "uint16"),
+    "ip": sb(32, "int32"), "ia": sb(32, "int32"), "ic": sb(32, "int32"), "base": sb(32, "float32"), "wo": sb(32 * N, "uint16"),
+    "pl": sb(32, "int32"), "ofl": sb(32, "int32"), "i1": sb(32, "float32"), "i2": sb(32, "float32"), "idx": sb(32, "uint16"),
+    "xt": sb(4 * TC, "bfloat16"), "xg": sb(4 * SLOTS, "bfloat16"), "xq": sb(SLOTS, CODE), "xs": sb(SLOTS, "uint8"),
+    "wt": sb(8 * NE, "bfloat16"), "wg": sb(4 * NE * N, "bfloat16"), "wq": sb(NE * N, CODE), "ws": sb(NE * N, "uint8"),
+    "xr": sb(SLOTS, CODE), "xrs": sb(SLOTS, "uint8"), "ew": sb(NE * N, CODE), "es": sb(NE * N, "uint8"),
+    "hx": sb(2 * CAPP, CODE), "hxs": sb(2 * CAPP, "uint8"), "hw": sb(2 * NE, CODE), "hws": sb(2 * NE, "uint8"),
+    "ps": ("psum", [128, 4096], "float32"), "res": sb(N * SLOTS, "float32"), "yt": sb(TC, "float32"),
 }
-SEMAPHORES = (["ldsel", "ldsnd", "ldx", "ldw", "ldi", "rep", "own", "yd",
-               "iot", "ian", "bas", "selb", "sfd", "selq", "seli", "xoa", "xob", "xga", "xgb", "xqa", "xqb",
-               "ix1", "ix2", "ix3", "woa", "wob", "woc", "wga", "wgb", "wgc", "wqa", "wqb", "wqc",
-               "xin", "cpl", "gv", "gs", "sent", "hxc", "hxp", "hwc", "hwp"]
-              + ["we%d" % k for k in range(N)] + ["ma%d" % k for k in range(N)] + ["mb%d" % k for k in range(N)]
-              + ["cp%d" % k for k in range(4)])
+SEMAPHORES = (["ldsel", "ldsnd", "ldx", "ldw", "ldi", "rep", "own", "yd", "iot", "ian", "bas", "selb", "sfd",
+               "selq", "seli", "selo", "ix1", "ix2", "ix3", "xin", "cpl", "gv", "gs", "sent", "hxc", "hxp", "hwc", "hwp"]
+              + [a + b for a in ("xo", "xg", "xq") for b in "01"] + [a + b for a in ("wo", "wg", "wq") for b in "QSPO"]
+              + [a + "%d" % k for a in ("we", "ma", "mb") for k in range(N)] + ["cp%d" % k for k in range(4)])
 
 
 def bits(es):
@@ -60,45 +55,31 @@ def plan(core, T, topo):
     return p
 
 
-def dst_of(topo, c):
+def tx(topo, c, mask, rs, src, dst):
     rid, pid, _ = topo.addr(c)
-    return DstId(rid=rid, pnc=pid)
-
-
-def u8(ap):
-    return ap.bitcast(dt.uint8)
+    if src.dtype == dt.float8_e4m3fn_x4:
+        src, dst = src.bitcast(dt.uint8), dst.bitcast(dt.uint8)
+    return RemoteDMATransfer(dst_ids=[DstId(rid=rid, pnc=pid)], dma_engine_mask=mask, remote_sem=rs, src=src, dst=dst)
 
 
 def helper_program(g, core, T, topo):
     for r in range(N):
         p = plan(T.cores[r], T, topo)
-        if core == p["A"]:
-            pair, both = p["Q"], True
-        elif core == p["B"]:
-            pair, both = p["S"], False
-        else:
+        if core not in (p["A"], p["B"]):
             continue
+        pair = p["Q"] if core == p["A"] else p["S"]
         off = topo.engines(core, T.cores[pair[0]])
         h = len(off) // 2
-        masks = [bits(off[:h]), bits(off[h:])]
-        count = [0]
-
-        def hand(sem, n, src, w, dst, at, rsem, code):
-            g.wait_ge(sem, n)
-            view = u8 if code else (lambda v: v)
-            g.remote_dma_fused([RemoteDMATransfer(
-                dst_ids=[dst_of(topo, T.cores[d])], dma_engine_mask=masks[i], remote_sem=rsem,
-                src=view(src[:, i * w:(i + 1) * w]), dst=view(dst[:, at * w:(at + 1) * w])) for i, d in enumerate(pair)],
-                local_sem=T.sem.sent)
-            count[0] += 2 * h
-
         on = len(topo.engines(core, T.cores[r])) - len(off)
-        hand(T.sem.hxc, on // 2, T.hx, CAPP, T.xr, r, T.sem.xin, True)
-        hand(T.sem.hxp, on // 2, T.hxs, CAPP, T.xrs, r, T.sem.xin, False)
-        if both:
-            hand(T.sem.hwc, on, T.hw, NE, T.ew, r, T.sem["we%d" % r], True)
-            hand(T.sem.hwp, on, T.hws, NE, T.es, r, T.sem["we%d" % r], False)
-        g.wait_ge(T.sem.sent, count[0])
+        we = T.sem["we%d" % r]
+        jobs = [(T.sem.hxc, on // 2, T.hx, CAPP, T.xr, T.sem.xin), (T.sem.hxp, on // 2, T.hxs, CAPP, T.xrs, T.sem.xin)]
+        if core == p["A"]:
+            jobs += [(T.sem.hwc, on, T.hw, NE, T.ew, we), (T.sem.hwp, on, T.hws, NE, T.es, we)]
+        for sem, n, src, w, dst, rs in jobs:
+            g.wait_ge(sem, n)
+            g.remote_dma_fused([tx(topo, T.cores[d], bits(off[i * h:i * h + h]), rs, src[:, i * w:(i + 1) * w],
+                                   dst[:, r * w:(r + 1) * w]) for i, d in enumerate(pair)], local_sem=T.sem.sent)
+        g.wait_ge(T.sem.sent, 2 * h * len(jobs))
 
 
 def rank_program(g, core, T, topo):
@@ -111,7 +92,7 @@ def rank_program(g, core, T, topo):
     cores = T.cores
     p = plan(core, T, topo)
     partner = [d for d in p["O"] if d != r][0]
-    order = p["Q"] + p["S"] + p["O"] + p["P"]
+    order = p["Q"] + p["S"] + p["P"] + p["O"]
     pos = {d: k for k, d in enumerate(order)}
     off = topo.engines(core, cores[p["P"][0]])
     on = [e for e in topo.engines(core, cores[partner]) if e not in off]
@@ -119,11 +100,11 @@ def rank_program(g, core, T, topo):
     offm, onm = [bits(off[:o4]), bits(off[o4:])], [bits(on[:n4]), bits(on[n4:])]
 
     Y.dma_start(T.srow[0:1, :], T.sel[:]).then_inc(sem.ldsel, 16)
+    Y.dma_start(T.xt[0:64, :], T.x[0:64, :]).then_inc(sem.ldx, 16)
+    S.dma_start(T.xt[64:128, :], T.x[64:128, :]).then_inc(sem.ldx, 16)
     for k in range(8):
         q = Y if k % 2 else S
         q.dma_start(T.snd[16 * k:16 * k + 16, :], T.send[:]).then_inc(sem.ldsnd, 16)
-    Y.dma_start(T.xt[0:64, :], T.x[0:64, :]).then_inc(sem.ldx, 16)
-    S.dma_start(T.xt[64:128, :], T.x[64:128, :]).then_inc(sem.ldx, 16)
     Y.dma_start(T.wt[:, 0:4 * NE], T.w[0:128, :]).then_inc(sem.ldw, 16)
     S.dma_start(T.wt[:, 4 * NE:8 * NE], T.w[128:256, :]).then_inc(sem.ldw, 16)
     Y.dma_start(T.pl[0:16, :], T.place[:]).then_inc(sem.ldi, 16)
@@ -142,45 +123,66 @@ def rank_program(g, core, T, topo):
     V.tensor_scalar(T.sf[:], T.sbc[:], float(4 * NE), 0.0, A.mult, A.max).then_inc(sem.sfd, 1)
 
     sent = 0
-    tr = []
-    share = {d: [e] for d, e in zip(p["S"] + p["Q"], off[0:4])}
-    share.update({d: off[4 + 2 * i:6 + 2 * i] for i, d in enumerate(p["P"])})
-    share[partner] = on
-    for d in p["P"] + p["S"] + p["Q"] + [partner]:
-        first = r in plan(cores[d], T, topo)["Q"]
-        tr.append(RemoteDMATransfer(dst_ids=[dst_of(topo, cores[d])], dma_engine_mask=bits(share[d]),
-                                    remote_sem=sem.selq if first else sem.seli,
-                                    src=T.sf[:, d:d + 1], dst=T.selv[:, r:r + 1]))
-        sent += len(share[d])
     g.wait_ge(sem.sfd, 1)
-    g.remote_dma_fused(tr, local_sem=sem.sent)
-    nq, ni = 2 * 2, 4 * 1 + len(on)
+    two = [(d, off[2 * i:2 * i + 2], sem.seli) for i, d in enumerate(p["S"] + p["Q"])] + [(partner, on[:2], sem.selo)]
+    for call in ([(d, off[o4 * i:o4 * i + o4], sem.selq) for i, d in enumerate(p["P"])], two):
+        g.remote_dma_fused([tx(topo, cores[d], bits(es), s, T.sf[:, d:d + 1], T.selv[:, r:r + 1]) for d, es, s in call],
+                           local_sem=sem.sent)
+        sent += sum(len(es) for _, es, _ in call)
+    arrive = {"Q": (sem.selq, 2 * o4), "S": (sem.seli, 4 * 2), "O": (sem.selo, 2)}
 
     V.wait_ge(sem.ldsnd, 128)
     for k in range(4):
         d = order[2 * k]
         V.tensor_scalar(T.xo[:, 12 * k:12 * k + 12], T.snd[:, 6 * d:6 * d + 12], 4.0, 0.0, A.mult, A.max
-                        ).then_inc(sem.xoa if k < 2 else sem.xob, 1)
-    for q, ts in ((V, (0, 1)), (S, (2, 3))):
+                        ).then_inc(sem["xo%d" % (k // 2)], 1)
+
+    def gather(q, a, b, t, s):
+        out, win = T.xg[:, 4 * a + t:4 * b:4], T.xt[:, t:4 * TC].indirect(T.xo[:, a // 16:b // 16])
+        (V.tensor_copy(out, win) if q is V else S.activation(out, win, COPY)).then_inc(s, 1)
+
+    for q in (V, S):
         q.wait_ge(sem.ldx, 32)
-        for b, (so, sg, sq) in enumerate(((sem.xoa, sem.xga, sem.xqa), (sem.xob, sem.xgb, sem.xqb))):
-            a = HALF * b
-            q.wait_ge(so, 2)
-            for t in ts:
-                out = T.xg[:, 4 * a + t:4 * (a + HALF):4]
-                win = T.xt[:, t:4 * TC].indirect(T.xo[:, a // 16:(a + HALF) // 16])
-                if q is V:
-                    V.tensor_copy(out, win).then_inc(sg, 1)
-                else:
-                    S.activation(out, win, COPY).then_inc(sg, 1)
+        for b in range(2):
+            a, e, s = HALF * b, HALF * (b + 1), sem["xg%d" % b]
+            c = e - (128 if b else 0)
+            q.wait_ge(sem["xo%d" % b], 2)
+            for (lo, hi, t) in (((a, e, 0), (a, c, 1)) if q is V else ((a, e, 2), (a, e, 3), (c, e, 1))):
+                if lo < hi:
+                    gather(q, lo, hi, t, s)
             if q is V:
-                V.wait_ge(sg, 4)
-                V.quantize_mx(T.xq[:, a:a + HALF], T.xs[:, a:a + HALF], T.xg[:, 4 * a:4 * (a + HALF)]).then_inc(sq, 1)
+                V.wait_ge(s, 4 + b)
+                V.quantize_mx(T.xq[:, a:e], T.xs[:, a:e], T.xg[:, 4 * a:4 * e]).then_inc(sem["xq%d" % b], 1)
 
     a = CAPP * pos[r]
-    Y.wait_ge(sem.xqb, 1)
-    Y.dma_start(u8(T.xr[:, CAPP * r:CAPP * (r + 1)]), u8(T.xq[:, a:a + CAPP])).then_inc(sem.own, 16)
+    Y.wait_ge(sem.xq1, 1)
+    Y.dma_start(T.xr[:, CAPP * r:CAPP * (r + 1)].bitcast(dt.uint8), T.xq[:, a:a + CAPP].bitcast(dt.uint8)).then_inc(sem.own, 16)
     Y.dma_start(T.xrs[:, CAPP * r:CAPP * (r + 1)], T.xs[:, a:a + CAPP]).then_inc(sem.own, 16)
+
+    def offs(c):
+        for d in p[c]:
+            col = T.sf[:, r:r + 1] if d == r else T.selv[:, d:d + 1]
+            V.tensor_scalar(T.wo[:, 32 * pos[d]:32 * pos[d] + 32], T.base[:], col, None, A.add).then_inc(sem["wo" + c], 1)
+
+    V.wait_ge(sem.bas, 1)
+    V.wait_ge(sem.ldw, 32)
+    S.wait_ge(sem.ldw, 32)
+    for k, (c, share) in enumerate((("Q", 512), ("S", 512), ("P", 384), ("O", 416))):
+        a, m, e = 1024 * k, 1024 * k + share, 1024 * (k + 1)
+        wo, wg = sem["wo" + c], sem["wg" + c]
+        if c in "QS":
+            V.wait_ge(*arrive[c])
+            offs(c)
+        S.wait_ge(wo, 2)
+        S.activation(T.wg[:, m:e], T.wt[:].indirect(T.wo[:, m // 16:e // 16]), COPY).then_inc(wg, 1)
+        V.wait_ge(wo, 2)
+        V.tensor_copy(T.wg[:, a:m], T.wt[:].indirect(T.wo[:, a // 16:m // 16])).then_inc(wg, 1)
+        if c == "S":
+            offs("P")
+            V.wait_ge(*arrive["O"])
+            offs("O")
+        V.wait_ge(wg, 2)
+        V.quantize_mx(T.wq[:, a // 4:e // 4], T.ws[:, a // 4:e // 4], T.wg[:, a:e]).then_inc(sem["wq" + c], 1)
 
     V.wait_ge(sem.ldi, 32)
     V.tensor_scalar(T.i1[0:16, :], T.ofl[0:16, :], float(SLOTS), None, A.mult).then_inc(sem.ix1, 1)
@@ -192,88 +194,38 @@ def rank_program(g, core, T, topo):
     for k in range(1, 8):
         Y.dma_start(T.idx[16 * k:16 * k + 16, :], T.idx[0:16, :]).then_inc(sem.rep, 16)
 
-    def offs(d, s):
-        col = T.sf[:, r:r + 1] if d == r else T.selv[:, d:d + 1]
-        k = pos[d]
-        V.tensor_scalar(T.wo[:, 32 * k:32 * k + 32], T.base[:], col, None, A.add).then_inc(s, 1)
+    def send(items):
+        for i in (0, 1):
+            g.remote_dma_fused([tx(topo, c, m, s[i], src[i][:, lo:hi], dst[i]) for c, m, s, src, lo, hi, dst in items],
+                               local_sem=sem.sent)
+        return 2 * sum(bin(m).count("1") for _, m, *_ in items)
 
-    def pick(q, ks, s):
-        out = T.wg[:, 4 * NE * ks[0]:4 * NE * (ks[-1] + 1)]
-        win = T.wt[:].indirect(T.wo[:, 32 * ks[0]:32 * (ks[-1] + 1)])
-        if q is V:
-            V.tensor_copy(out, win).then_inc(s, 1)
-        else:
-            S.activation(out, win, COPY).then_inc(s, 1)
+    def direct(d, m, w):
+        src, dst, s = (((T.xq, T.xs), (T.xr, T.xrs), sem.xin) if w == CAPP else ((T.wq, T.ws), (T.ew, T.es), sem["we%d" % r]))
+        return (cores[d], m, (s, s), src, w * pos[d], w * (pos[d] + 1), [t[:, w * r:w * (r + 1)] for t in dst])
 
-    def pack(k, n, s):
-        V.quantize_mx(T.wq[:, NE * k:NE * (k + n)], T.ws[:, NE * k:NE * (k + n)],
-                      T.wg[:, 4 * NE * k:4 * NE * (k + n)]).then_inc(s, 1)
+    def help_x(h, c, m):
+        return (p[h], m, (sem.hxc, sem.hxp), (T.xq, T.xs), CAPP * pos[p[c][0]], CAPP * (pos[p[c][0]] + 2), (T.hx[:], T.hxs[:]))
 
-    V.wait_ge(sem.bas, 1)
-    V.wait_ge(sem.ldw, 32)
-    S.wait_ge(sem.ldw, 32)
-    V.wait_ge(sem.selq, nq)
-    for (vk, sk, so, sg, sq) in (([0], [1], sem.woa, sem.wga, sem.wqa), ([2, 3], [4, 5], sem.wob, sem.wgb, sem.wqb),
-                                 ([6], [7], sem.woc, sem.wgc, sem.wqc)):
-        for k in sk + vk:
-            offs(order[k], so)
-        n = len(vk + sk)
-        S.wait_ge(so, n)
-        pick(S, sk, sg)
-        V.wait_ge(so, n)
-        pick(V, vk, sg)
-        V.wait_ge(sg, 2)
-        pack(vk[0], n, sq)
-        if n == 2 and vk[0] == 0:
-            V.wait_ge(sem.seli, ni)
-
-    def send(items, local):
-        g.remote_dma_fused(items, local_sem=local)
-
-    def tx(c, mask, rs, src, dst):
-        return RemoteDMATransfer(dst_ids=[dst_of(topo, c)], dma_engine_mask=mask, remote_sem=rs, src=src, dst=dst)
-
-    def xcol(d, n=1):
-        return CAPP * pos[d], CAPP * (pos[d] + n)
-
-    x0, x1 = xcol(p["Q"][0], 2)
-    z0, z1 = xcol(p["S"][0], 2)
-    g.wait_ge(sem.xqa, 1)
-    send([tx(p["A"], onm[0], sem.hxc, u8(T.xq[:, x0:x1]), u8(T.hx[:])),
-          tx(p["B"], onm[1], sem.hxc, u8(T.xq[:, z0:z1]), u8(T.hx[:]))], sem.sent)
-    send([tx(p["A"], onm[0], sem.hxp, T.xs[:, x0:x1], T.hxs[:]),
-          tx(p["B"], onm[1], sem.hxp, T.xs[:, z0:z1], T.hxs[:])], sem.sent)
-    sent += 2 * len(on)
-
-    def spread(pair, withp, src, ssrc, dst, sdst, w, rs):
-        tgt = [(d, offm[i]) for i, d in enumerate(pair)] + ([(partner, bits(on))] if withp else [])
-        for code in (True, False):
-            view = u8 if code else (lambda v: v)
-            s, t = (src, dst) if code else (ssrc, sdst)
-            send([tx(cores[d], m, rs, view(s[:, w * pos[d]:w * (pos[d] + 1)]), view(t[:, w * r:w * (r + 1)]))
-                  for d, m in tgt], sem.sent)
-        return 2 * (len(off) + (len(on) if withp else 0))
-
-    g.wait_ge(sem.xqb, 1)
-    sent += spread(p["P"], True, T.xq, T.xs, T.xr, T.xrs, CAPP, sem.xin)
-    we = sem["we%d" % r]
-    g.wait_ge(sem.wqa, 1)
-    k = NE * pos[p["Q"][0]]
-    send([tx(p["A"], bits(on), sem.hwc, u8(T.wq[:, k:k + 2 * NE]), u8(T.hw[:]))], sem.sent)
-    send([tx(p["A"], bits(on), sem.hwp, T.ws[:, k:k + 2 * NE], T.hws[:])], sem.sent)
-    sent += 2 * len(on)
-    g.wait_ge(sem.wqb, 1)
-    sent += spread(p["S"], True, T.wq, T.ws, T.ew, T.es, NE, we)
-    g.wait_ge(sem.wqc, 1)
-    sent += spread(p["P"], False, T.wq, T.ws, T.ew, T.es, NE, we)
+    g.wait_ge(sem.xq0, 1)
+    sent += send([help_x("A", "Q", onm[0]), help_x("B", "S", onm[1])])
+    g.wait_ge(sem.xq1, 1)
+    sent += send([direct(d, offm[i], CAPP) for i, d in enumerate(p["P"])] + [direct(partner, bits(on), CAPP)])
+    g.wait_ge(sem.wqQ, 1)
+    sent += send([(p["A"], bits(on), (sem.hwc, sem.hwp), (T.wq, T.ws), 0, 2 * NE, (T.hw[:], T.hws[:]))])
+    for c in "SP":
+        g.wait_ge(sem["wq" + c], 1)
+        sent += send([direct(d, offm[i], NE) for i, d in enumerate(p[c])])
+    g.wait_ge(sem.wqO, 1)
+    sent += send([direct(partner, bits(on), NE)])
     g.wait_ge(sem.sent, sent)
 
-    todo = [r, partner] + p["S"] + p["Q"] + p["P"]
+    todo = [r] + p["S"] + [partner] + p["Q"] + p["P"]
     PE.wait_ge(sem.own, 32)
     PE.wait_ge(sem.xin, 6 * 2 * o4 + 2 * len(on))
     for k, h in enumerate(todo):
         if h == r:
-            PE.wait_ge(sem.wqb, 1)
+            PE.wait_ge(sem.wqO, 1)
             st, ss = T.wq[:, NE * pos[r]:NE * (pos[r] + 1)], T.ws[:, NE * pos[r]:NE * (pos[r] + 1)]
         else:
             PE.wait_ge(sem["we%d" % h], 2 * (len(on) if h == partner else o4))
@@ -281,15 +233,14 @@ def rank_program(g, core, T, topo):
         if k >= 4:
             PE.wait_ge(sem["cp%d" % (k - 4)], 2)
         b = 1024 * (k % 4)
-        PE.matmul_mx(T.ps[:, b:b + HALF], st, ss, T.xr[:, 0:HALF], T.xrs[:, 0:HALF], True, True
-                     ).then_inc(sem["ma%d" % k], 1)
-        PE.matmul_mx(T.ps[:, b + 512:b + 512 + HALF], st, ss, T.xr[:, HALF:SLOTS], T.xrs[:, HALF:SLOTS], True, True
-                     ).then_inc(sem["mb%d" % k], 1)
         done = sem["cp%d" % k] if k < 4 else sem.cpl
-        V.wait_ge(sem["ma%d" % k], 1)
-        V.tensor_copy(T.res[:, SLOTS * h:SLOTS * h + HALF], T.ps[:, b:b + HALF]).then_inc(done, 1)
-        S.wait_ge(sem["mb%d" % k], 1)
-        S.activation(T.res[:, SLOTS * h + HALF:SLOTS * (h + 1)], T.ps[:, b + 512:b + 512 + HALF], COPY).then_inc(done, 1)
+        for i, s in enumerate((sem["ma%d" % k], sem["mb%d" % k])):
+            x0, bank, out = HALF * i, T.ps[:, b + 512 * i:b + 512 * i + HALF], SLOTS * h + HALF * i
+            PE.matmul_mx(bank, st, ss, T.xr[:, x0:x0 + HALF], T.xrs[:, x0:x0 + HALF], True, True).then_inc(s, 1)
+            q = S if i else V
+            q.wait_ge(s, 1)
+            o = T.res[:, out:out + HALF]
+            (S.activation(o, bank, COPY) if i else V.tensor_copy(o, bank)).then_inc(done, 1)
 
     h = TC // 2
     for q in (V, S):

from concourse.bass import DstId, RemoteDMATransfer
from concourse.mybir import dt, AluOpType, ActivationFunctionType

N, TC, CAPP, NE = 8, 512, 96, 128
SLOTS = N * CAPP
HALF = SLOTS // 2
CODE = "float8_e4m3fn_x4"


def sb(n, t, p=128):
    return ("sbuf", [p, n], t)


SCRATCH = {
    "srow": sb(16, "int32", 1), "sbc": sb(16, "int32"), "sf": sb(16, "float32"), "selv": sb(N, "float32"),
    "snd": sb(SLOTS // 16, "int32"), "xo": sb(SLOTS // 16, "uint16"),
    "ip": sb(32, "int32"), "ia": sb(32, "int32"), "ic": sb(32, "int32"), "base": sb(32, "float32"), "wo": sb(32 * N, "uint16"),
    "pl": sb(32, "int32"), "ofl": sb(32, "int32"), "i1": sb(32, "float32"), "i2": sb(32, "float32"), "idx": sb(32, "uint16"),
    "xt": sb(4 * TC, "bfloat16"), "xg": sb(4 * SLOTS, "bfloat16"), "xq": sb(SLOTS, CODE), "xs": sb(SLOTS, "uint8"),
    "wt": sb(8 * NE, "bfloat16"), "wg": sb(4 * NE * N, "bfloat16"), "wq": sb(NE * N, CODE), "ws": sb(NE * N, "uint8"),
    "xr": sb(SLOTS, CODE), "xrs": sb(SLOTS, "uint8"), "ew": sb(NE * N, CODE), "es": sb(NE * N, "uint8"),
    "hx": sb(2 * CAPP, CODE), "hxs": sb(2 * CAPP, "uint8"), "hw": sb(2 * NE, CODE), "hws": sb(2 * NE, "uint8"),
    "ps": ("psum", [128, 4096], "float32"), "res": sb(N * SLOTS, "float32"), "yt": sb(TC, "float32"),
}
SEMAPHORES = (["ldsel", "ldsnd", "ldx", "ldw", "ldi", "rep", "own", "yd", "iot", "ian", "bas", "selb", "sfd",
               "selq", "seli", "selo", "ix1", "ix2", "ix3", "xin", "cpl", "gv", "gs", "sent", "hxc", "hxp", "hwc", "hwp"]
              + [a + b for a in ("xo", "xg", "xq") for b in "01"] + [a + b for a in ("wo", "wg", "wq") for b in "QSPO"]
              + [a + "%d" % k for a in ("we", "ma", "mb") for k in range(N)] + ["cp%d" % k for k in range(4)])


def bits(es):
    m = 0
    for e in es:
        m |= 1 << e
    return m


def plan(core, T, topo):
    cores = list(T.cores)
    chips = []
    for c in cores:
        if topo.chip(c) not in chips:
            chips.append(topo.chip(c))
    pair = [[r for r in range(N) if topo.chip(cores[r]) == h] for h in chips]
    k = chips.index(topo.chip(core))
    rest = [(k + i) % len(chips) for i in range(1, len(chips))]
    same = [i for i in rest if topo.same_plane(chips[i], chips[k])]
    cross = [i for i in rest if i not in same]
    p = {"O": pair[k], "S": pair[same[0]], "P": pair[cross[0]], "Q": pair[cross[1]]}
    mine = pair[k].index(T.rank_of(core))
    away = [c for c in topo.cores_of(core) if c not in cores and topo.die(c) != topo.die(core)]
    owners = [c for c in away if all(topo.may_write(c, cores[d]) for d in p["Q"])]
    p["A"] = owners[mine]
    p["B"] = [c for c in away if c not in owners][mine]
    return p


def tx(topo, c, mask, rs, src, dst):
    rid, pid, _ = topo.addr(c)
    if src.dtype == dt.float8_e4m3fn_x4:
        src, dst = src.bitcast(dt.uint8), dst.bitcast(dt.uint8)
    return RemoteDMATransfer(dst_ids=[DstId(rid=rid, pnc=pid)], dma_engine_mask=mask, remote_sem=rs, src=src, dst=dst)


def helper_program(g, core, T, topo):
    for r in range(N):
        p = plan(T.cores[r], T, topo)
        if core not in (p["A"], p["B"]):
            continue
        pair = p["Q"] if core == p["A"] else p["S"]
        off = topo.engines(core, T.cores[pair[0]])
        h = len(off) // 2
        on = len(topo.engines(core, T.cores[r])) - len(off)
        we = T.sem["we%d" % r]
        jobs = [(T.sem.hxc, on // 2, T.hx, CAPP, T.xr, T.sem.xin), (T.sem.hxp, on // 2, T.hxs, CAPP, T.xrs, T.sem.xin)]
        if core == p["A"]:
            jobs += [(T.sem.hwc, on, T.hw, NE, T.ew, we), (T.sem.hwp, on, T.hws, NE, T.es, we)]
        for sem, n, src, w, dst, rs in jobs:
            g.wait_ge(sem, n)
            g.remote_dma_fused([tx(topo, T.cores[d], bits(off[i * h:i * h + h]), rs, src[:, i * w:(i + 1) * w],
                                   dst[:, r * w:(r + 1) * w]) for i, d in enumerate(pair)], local_sem=T.sem.sent)
        g.wait_ge(T.sem.sent, 2 * h * len(jobs))


def rank_program(g, core, T, topo):
    r = T.rank_of(core)
    if r is None:
        return helper_program(g, core, T, topo)
    V, S, PE, Y = g.vector, g.scalar, g.tensor, g.sync
    sem, A = T.sem, AluOpType
    COPY = ActivationFunctionType.Copy
    cores = T.cores
    p = plan(core, T, topo)
    partner = [d for d in p["O"] if d != r][0]
    order = p["Q"] + p["S"] + p["P"] + p["O"]
    pos = {d: k for k, d in enumerate(order)}
    off = topo.engines(core, cores[p["P"][0]])
    on = [e for e in topo.engines(core, cores[partner]) if e not in off]
    o4, n4 = len(off) // 2, len(on) // 2
    offm, onm = [bits(off[:o4]), bits(off[o4:])], [bits(on[:n4]), bits(on[n4:])]

    Y.dma_start(T.srow[0:1, :], T.sel[:]).then_inc(sem.ldsel, 16)
    Y.dma_start(T.xt[0:64, :], T.x[0:64, :]).then_inc(sem.ldx, 16)
    S.dma_start(T.xt[64:128, :], T.x[64:128, :]).then_inc(sem.ldx, 16)
    for k in range(8):
        q = Y if k % 2 else S
        q.dma_start(T.snd[16 * k:16 * k + 16, :], T.send[:]).then_inc(sem.ldsnd, 16)
    Y.dma_start(T.wt[:, 0:4 * NE], T.w[0:128, :]).then_inc(sem.ldw, 16)
    S.dma_start(T.wt[:, 4 * NE:8 * NE], T.w[128:256, :]).then_inc(sem.ldw, 16)
    Y.dma_start(T.pl[0:16, :], T.place[:]).then_inc(sem.ldi, 16)
    Y.dma_start(T.ofl[0:16, :], T.of[:]).then_inc(sem.ldi, 16)

    g.iota(T.ip[:], [[0, 32]], 0, 1).then_inc(sem.iot, 1)
    g.iota(T.ic[:], [[16, 32]], 0, 0).then_inc(sem.iot, 1)
    g.wait_ge(sem.ldsel, 16)
    g.partition_broadcast(T.sbc[:], T.srow[0:1, :], 128).then_inc(sem.selb, 1)

    V.wait_ge(sem.iot, 2)
    V.tensor_scalar(T.ia[:], T.ip[:], 15, None, A.bitwise_and).then_inc(sem.ian, 1)
    V.wait_ge(sem.ian, 1)
    V.tensor_tensor(T.base[:], T.ia[:], T.ic[:], A.add).then_inc(sem.bas, 1)
    V.wait_ge(sem.selb, 1)
    V.tensor_scalar(T.sf[:], T.sbc[:], float(4 * NE), 0.0, A.mult, A.max).then_inc(sem.sfd, 1)

    sent = 0
    g.wait_ge(sem.sfd, 1)
    two = [(d, off[2 * i:2 * i + 2], sem.seli) for i, d in enumerate(p["S"] + p["Q"])] + [(partner, on[:2], sem.selo)]
    for call in ([(d, off[o4 * i:o4 * i + o4], sem.selq) for i, d in enumerate(p["P"])], two):
        g.remote_dma_fused([tx(topo, cores[d], bits(es), s, T.sf[:, d:d + 1], T.selv[:, r:r + 1]) for d, es, s in call],
                           local_sem=sem.sent)
        sent += sum(len(es) for _, es, _ in call)
    arrive = {"Q": (sem.selq, 2 * o4), "S": (sem.seli, 4 * 2), "O": (sem.selo, 2)}

    V.wait_ge(sem.ldsnd, 128)
    for k in range(4):
        d = order[2 * k]
        V.tensor_scalar(T.xo[:, 12 * k:12 * k + 12], T.snd[:, 6 * d:6 * d + 12], 4.0, 0.0, A.mult, A.max
                        ).then_inc(sem["xo%d" % (k // 2)], 1)

    def gather(q, a, b, t, s):
        out, win = T.xg[:, 4 * a + t:4 * b:4], T.xt[:, t:4 * TC].indirect(T.xo[:, a // 16:b // 16])
        (V.tensor_copy(out, win) if q is V else S.activation(out, win, COPY)).then_inc(s, 1)

    for q in (V, S):
        q.wait_ge(sem.ldx, 32)
        for b in range(2):
            a, e, s = HALF * b, HALF * (b + 1), sem["xg%d" % b]
            c = e - (128 if b else 0)
            q.wait_ge(sem["xo%d" % b], 2)
            for (lo, hi, t) in (((a, e, 0), (a, c, 1)) if q is V else ((a, e, 2), (a, e, 3), (c, e, 1))):
                if lo < hi:
                    gather(q, lo, hi, t, s)
            if q is V:
                V.wait_ge(s, 4 + b)
                V.quantize_mx(T.xq[:, a:e], T.xs[:, a:e], T.xg[:, 4 * a:4 * e]).then_inc(sem["xq%d" % b], 1)

    a = CAPP * pos[r]
    Y.wait_ge(sem.xq1, 1)
    Y.dma_start(T.xr[:, CAPP * r:CAPP * (r + 1)].bitcast(dt.uint8), T.xq[:, a:a + CAPP].bitcast(dt.uint8)).then_inc(sem.own, 16)
    Y.dma_start(T.xrs[:, CAPP * r:CAPP * (r + 1)], T.xs[:, a:a + CAPP]).then_inc(sem.own, 16)

    def offs(c):
        for d in p[c]:
            col = T.sf[:, r:r + 1] if d == r else T.selv[:, d:d + 1]
            V.tensor_scalar(T.wo[:, 32 * pos[d]:32 * pos[d] + 32], T.base[:], col, None, A.add).then_inc(sem["wo" + c], 1)

    V.wait_ge(sem.bas, 1)
    V.wait_ge(sem.ldw, 32)
    S.wait_ge(sem.ldw, 32)
    for k, (c, share) in enumerate((("Q", 512), ("S", 512), ("P", 384), ("O", 416))):
        a, m, e = 1024 * k, 1024 * k + share, 1024 * (k + 1)
        wo, wg = sem["wo" + c], sem["wg" + c]
        if c in "QS":
            V.wait_ge(*arrive[c])
            offs(c)
        S.wait_ge(wo, 2)
        S.activation(T.wg[:, m:e], T.wt[:].indirect(T.wo[:, m // 16:e // 16]), COPY).then_inc(wg, 1)
        V.wait_ge(wo, 2)
        V.tensor_copy(T.wg[:, a:m], T.wt[:].indirect(T.wo[:, a // 16:m // 16])).then_inc(wg, 1)
        if c == "S":
            offs("P")
            V.wait_ge(*arrive["O"])
            offs("O")
        V.wait_ge(wg, 2)
        V.quantize_mx(T.wq[:, a // 4:e // 4], T.ws[:, a // 4:e // 4], T.wg[:, a:e]).then_inc(sem["wq" + c], 1)

    V.wait_ge(sem.ldi, 32)
    V.tensor_scalar(T.i1[0:16, :], T.ofl[0:16, :], float(SLOTS), None, A.mult).then_inc(sem.ix1, 1)
    V.wait_ge(sem.ix1, 1)
    V.tensor_tensor(T.i2[0:16, :], T.i1[0:16, :], T.pl[0:16, :], A.add).then_inc(sem.ix2, 1)
    V.wait_ge(sem.ix2, 1)
    V.tensor_copy(T.idx[0:16, :], T.i2[0:16, :]).then_inc(sem.ix3, 1)
    Y.wait_ge(sem.ix3, 1)
    for k in range(1, 8):
        Y.dma_start(T.idx[16 * k:16 * k + 16, :], T.idx[0:16, :]).then_inc(sem.rep, 16)

    def send(items):
        for i in (0, 1):
            g.remote_dma_fused([tx(topo, c, m, s[i], src[i][:, lo:hi], dst[i]) for c, m, s, src, lo, hi, dst in items],
                               local_sem=sem.sent)
        return 2 * sum(bin(m).count("1") for _, m, *_ in items)

    def direct(d, m, w):
        src, dst, s = (((T.xq, T.xs), (T.xr, T.xrs), sem.xin) if w == CAPP else ((T.wq, T.ws), (T.ew, T.es), sem["we%d" % r]))
        return (cores[d], m, (s, s), src, w * pos[d], w * (pos[d] + 1), [t[:, w * r:w * (r + 1)] for t in dst])

    def help_x(h, c, m):
        return (p[h], m, (sem.hxc, sem.hxp), (T.xq, T.xs), CAPP * pos[p[c][0]], CAPP * (pos[p[c][0]] + 2), (T.hx[:], T.hxs[:]))

    g.wait_ge(sem.xq0, 1)
    sent += send([help_x("A", "Q", onm[0]), help_x("B", "S", onm[1])])
    g.wait_ge(sem.xq1, 1)
    sent += send([direct(d, offm[i], CAPP) for i, d in enumerate(p["P"])] + [direct(partner, bits(on), CAPP)])
    g.wait_ge(sem.wqQ, 1)
    sent += send([(p["A"], bits(on), (sem.hwc, sem.hwp), (T.wq, T.ws), 0, 2 * NE, (T.hw[:], T.hws[:]))])
    for c in "SP":
        g.wait_ge(sem["wq" + c], 1)
        sent += send([direct(d, offm[i], NE) for i, d in enumerate(p[c])])
    g.wait_ge(sem.wqO, 1)
    sent += send([direct(partner, bits(on), NE)])
    g.wait_ge(sem.sent, sent)

    todo = [r] + p["S"] + [partner] + p["Q"] + p["P"]
    PE.wait_ge(sem.own, 32)
    PE.wait_ge(sem.xin, 6 * 2 * o4 + 2 * len(on))
    for k, h in enumerate(todo):
        if h == r:
            PE.wait_ge(sem.wqO, 1)
            st, ss = T.wq[:, NE * pos[r]:NE * (pos[r] + 1)], T.ws[:, NE * pos[r]:NE * (pos[r] + 1)]
        else:
            PE.wait_ge(sem["we%d" % h], 2 * (len(on) if h == partner else o4))
            st, ss = T.ew[:, NE * h:NE * (h + 1)], T.es[:, NE * h:NE * (h + 1)]
        if k >= 4:
            PE.wait_ge(sem["cp%d" % (k - 4)], 2)
        b = 1024 * (k % 4)
        done = sem["cp%d" % k] if k < 4 else sem.cpl
        for i, s in enumerate((sem["ma%d" % k], sem["mb%d" % k])):
            x0, bank, out = HALF * i, T.ps[:, b + 512 * i:b + 512 * i + HALF], SLOTS * h + HALF * i
            PE.matmul_mx(bank, st, ss, T.xr[:, x0:x0 + HALF], T.xrs[:, x0:x0 + HALF], True, True).then_inc(s, 1)
            q = S if i else V
            q.wait_ge(s, 1)
            o = T.res[:, out:out + HALF]
            (S.activation(o, bank, COPY) if i else V.tensor_copy(o, bank)).then_inc(done, 1)

    h = TC // 2
    for q in (V, S):
        q.wait_ge(sem.rep, 112)
        q.wait_ge(sem.ix3, 1)
        q.wait_ge(sem.cpl, 8)
    V.tensor_copy(T.yt[:, 0:h], T.res[:].indirect(T.idx[:, 0:16])).then_inc(sem.gv, 1)
    S.activation(T.yt[:, h:TC], T.res[:].indirect(T.idx[:, 16:32]), COPY).then_inc(sem.gs, 1)
    Y.wait_ge(sem.gv, 1)
    Y.dma_start(T.y[:, 0:h], T.yt[:, 0:h]).then_inc(sem.yd, 16)
    S.wait_ge(sem.gs, 1)
    S.dma_start(T.y[:, h:TC], T.yt[:, h:TC]).then_inc(sem.yd, 16)
    Y.wait_ge(sem.yd, 32)
